import numpy as np
CORES = [64,65,66,67,68,69,70,71,72,73,74,75,76,77,78,79,80,81,82,83,84,85,86,87,88,89,90,91,92,93,94,95]
N = 32
ROOT = 27
def setup_inputs(rng):
    return {"x": rng.standard_normal((N, 128, N * 128), dtype=np.float32)}
def reference(x):
    return {"y": np.stack([x[ROOT][:, r * 128:(r + 1) * 128] for r in range(N)])}

@@ -1,0 +1,38 @@
+SCRATCH = {
+    "xs": ("sbuf", [128, 4096], "float32"),
+    "land": ("sbuf", [128, 128], "float32"),
+}
+SEMAPHORES = ["ld0", "ld1", "ld2", "ld3", "own", "read", "arrived", "stored"]
+
+B = 128
+
+
+def rank_program(g, core, T, topo):
+    rank = T.rank_of(core)
+    if rank is None:
+        return
+    root = T.cores[T.root]
+    if core != root:
+        n = 16 if topo.chip(core) == topo.chip(root) else 8
+        g.sync.wait_ge(T.sem.arrived, n)
+        g.sync.dma_start(T.y[:], T.land[:]).then_inc(T.sem.stored, 16)
+        g.sync.wait_ge(T.sem.stored, 16)
+        return
+    g.scalar.dma_start(T.y[:], T.x[:, T.root * B:(T.root + 1) * B]).then_inc(T.sem.own, 16)
+    order = [0, 1, 2, 3]
+    for i, k in enumerate(order):
+        q = g.sync if i % 2 == 0 else g.scalar
+        q.dma_start(T.xs[:, k * 8 * B:(k + 1) * 8 * B], T.x[:, k * 8 * B:(k + 1) * 8 * B]).then_inc(T.sem["ld%d" % k], 16)
+    sent = 0
+    for k in order:
+        g.wait_ge(T.sem["ld%d" % k], 16)
+        for r in range(8 * k, 8 * k + 8):
+            dst = T.cores[r]
+            if dst == core:
+                continue
+            rid, pid, _se = topo.addr(dst)
+            m = topo.mask(core, dst)
+            g.remote_dma(T.land[:], T.xs[:, r * B:(r + 1) * B], T.sem.arrived, T.sem.read, pid, rid, m)
+            sent += 16 if m == 0xFFFF else 8
+    g.wait_ge(T.sem.read, sent)
+    g.scalar.wait_ge(T.sem.own, 16)

@@ -1,10 +1,29 @@
-SCRATCH = {
-    "xs": ("sbuf", [128, 4096], "float32"),
-    "land": ("sbuf", [128, 128], "float32"),
-}
-SEMAPHORES = ["ld0", "ld1", "ld2", "ld3", "own", "read", "arrived", "stored"]
+from concourse.bass import DstId, RemoteDMATransfer
 
 B = 128
+Q = 4 * B
+C = 8 * B
+
+SCRATCH = {
+    "xs": ("sbuf", [128, 32 * B], "float32"),
+    "quad": ("sbuf", [128, Q], "float32"),
+    "land": ("sbuf", [128, B], "float32"),
+}
+SEMAPHORES = ["ld0", "ld1", "ld2", "ld3", "own", "chunk", "arrived", "read", "stored"]
+
+
+def middle_of(q, T, topo):
+    root = T.cores[T.root]
+    first = T.cores[4 * q]
+    if topo.chip(first) == topo.chip(root):
+        return None
+    if topo.die(first) == topo.die(root):
+        return first
+    others = [c for c in T.cores if topo.chip(c) == topo.chip(root) and topo.die(c) != topo.die(root)]
+    port = [c for c in others if topo.may_write(c, root ^ 8)]
+    if topo.same_plane(topo.chip(first), topo.chip(root)):
+        return [c for c in others if c not in port][0]
+    return port[0] if topo.mates(topo.chip(first), topo.chip(root)) else port[1]
 
 
 def rank_program(g, core, T, topo):
@@ -12,27 +31,65 @@ def rank_program(g, core, T, topo):
     if rank is None:
         return
     root = T.cores[T.root]
-    if core != root:
-        n = 16 if topo.chip(core) == topo.chip(root) else 8
-        g.sync.wait_ge(T.sem.arrived, n)
-        g.sync.dma_start(T.y[:], T.land[:]).then_inc(T.sem.stored, 16)
-        g.sync.wait_ge(T.sem.stored, 16)
+    mids = [middle_of(q, T, topo) for q in range(8)]
+
+    if core == root:
+        for k in range(4):
+            q = g.sync if k % 2 == 0 else g.scalar
+            q.dma_start(T.xs[:, k * C:(k + 1) * C], T.x[:, k * C:(k + 1) * C]).then_inc(T.sem["ld%d" % k], 16)
+        g.scalar.dma_start(T.y[:], T.x[:, rank * B:(rank + 1) * B]).then_inc(T.sem.own, 16)
+        left = 0
+        for k in range(4):
+            g.wait_ge(T.sem["ld%d" % k], 16)
+            if mids[2 * k] is not None:
+                trs = []
+                for q in (2 * k, 2 * k + 1):
+                    rid, pid, _se = topo.addr(mids[q])
+                    off_chip = topo.chip(mids[q]) != topo.chip(core)
+                    trs.append(RemoteDMATransfer(
+                        dst_ids=[DstId(rid=rid, pnc=pid)], dma_engine_mask=0x00FF if off_chip else 0xFF00,
+                        remote_sem=T.sem.chunk, src=T.xs[:, q * Q:(q + 1) * Q], dst=T.quad[:]))
+                    left += 8
+                g.remote_dma_fused(trs, local_sem=T.sem.read)
+            else:
+                for r in range(8 * k, 8 * k + 8):
+                    if r != rank:
+                        rid, pid, _se = topo.addr(T.cores[r])
+                        g.remote_dma(T.land[:], T.xs[:, r * B:(r + 1) * B], T.sem.arrived, T.sem.read, pid, rid, 0xFFFF)
+                        left += 16
+        g.wait_ge(T.sem.read, left)
+        g.scalar.wait_ge(T.sem.own, 16)
         return
-    g.scalar.dma_start(T.y[:], T.x[:, T.root * B:(T.root + 1) * B]).then_inc(T.sem.own, 16)
-    order = [0, 1, 2, 3]
-    for i, k in enumerate(order):
-        q = g.sync if i % 2 == 0 else g.scalar
-        q.dma_start(T.xs[:, k * 8 * B:(k + 1) * 8 * B], T.x[:, k * 8 * B:(k + 1) * 8 * B]).then_inc(T.sem["ld%d" % k], 16)
-    sent = 0
-    for k in order:
-        g.wait_ge(T.sem["ld%d" % k], 16)
-        for r in range(8 * k, 8 * k + 8):
-            dst = T.cores[r]
-            if dst == core:
-                continue
-            rid, pid, _se = topo.addr(dst)
-            m = topo.mask(core, dst)
-            g.remote_dma(T.land[:], T.xs[:, r * B:(r + 1) * B], T.sem.arrived, T.sem.read, pid, rid, m)
-            sent += 16 if m == 0xFFFF else 8
-    g.wait_ge(T.sem.read, sent)
-    g.scalar.wait_ge(T.sem.own, 16)
+
+    leader = False
+    if core in mids:
+        q = mids.index(core)
+        owners = [T.cores[r] for r in range(4 * q, 4 * q + 4)]
+        leader = core in owners
+        g.wait_ge(T.sem.chunk, 8)
+        if leader:
+            for j, dst in enumerate(owners):
+                if dst != core:
+                    rid, pid, _se = topo.addr(dst)
+                    g.remote_dma(T.land[:], T.quad[:, j * B:(j + 1) * B], T.sem.arrived, T.sem.read, pid, rid, 0xFFFF)
+            g.wait_ge(T.sem.read, 48)
+        else:
+            trs = []
+            for j, dst in enumerate(owners):
+                rid, pid, _se = topo.addr(dst)
+                trs.append(RemoteDMATransfer(
+                    dst_ids=[DstId(rid=rid, pnc=pid)], dma_engine_mask=0x3 << (2 * j),
+                    remote_sem=T.sem.arrived, src=T.quad[:, j * B:(j + 1) * B], dst=T.land[:]))
+            g.remote_dma_fused(trs, local_sem=T.sem.read)
+            g.wait_ge(T.sem.read, 8)
+
+    if leader:
+        j = rank % 4
+        g.sync.wait_ge(T.sem.chunk, 8)
+        g.sync.dma_start(T.y[:], T.quad[:, j * B:(j + 1) * B]).then_inc(T.sem.stored, 16)
+    else:
+        mid = mids[rank // 4]
+        on_chip = mid is None or topo.chip(mid) == topo.chip(core)
+        g.sync.wait_ge(T.sem.arrived, 16 if on_chip else 2)
+        g.sync.dma_start(T.y[:], T.land[:]).then_inc(T.sem.stored, 16)
+    g.sync.wait_ge(T.sem.stored, 16)

@@ -20,7 +20,8 @@ def middle_of(q, T, topo):
     if topo.die(first) == topo.die(root):
         return first
     others = [c for c in T.cores if topo.chip(c) == topo.chip(root) and topo.die(c) != topo.die(root)]
-    port = [c for c in others if topo.may_write(c, root ^ 8)]
+    on_mate = root ^ 8
+    port = [c for c in others if topo.may_write(c, on_mate)]
     if topo.same_plane(topo.chip(first), topo.chip(root)):
         return [c for c in others if c not in port][0]
     return port[0] if topo.mates(topo.chip(first), topo.chip(root)) else port[1]

from concourse.bass import DstId, RemoteDMATransfer

B = 128
Q = 4 * B
C = 8 * B

SCRATCH = {
    "xs": ("sbuf", [128, 32 * B], "float32"),
    "quad": ("sbuf", [128, Q], "float32"),
    "land": ("sbuf", [128, B], "float32"),
}
SEMAPHORES = ["ld0", "ld1", "ld2", "ld3", "own", "chunk", "arrived", "read", "stored"]


def middle_of(q, T, topo):
    root = T.cores[T.root]
    first = T.cores[4 * q]
    if topo.chip(first) == topo.chip(root):
        return None
    if topo.die(first) == topo.die(root):
        return first
    others = [c for c in T.cores if topo.chip(c) == topo.chip(root) and topo.die(c) != topo.die(root)]
    on_mate = root ^ 8
    port = [c for c in others if topo.may_write(c, on_mate)]
    if topo.same_plane(topo.chip(first), topo.chip(root)):
        return [c for c in others if c not in port][0]
    return port[0] if topo.mates(topo.chip(first), topo.chip(root)) else port[1]


def rank_program(g, core, T, topo):
    rank = T.rank_of(core)
    if rank is None:
        return
    root = T.cores[T.root]
    mids = [middle_of(q, T, topo) for q in range(8)]

    if core == root:
        for k in range(4):
            q = g.sync if k % 2 == 0 else g.scalar
            q.dma_start(T.xs[:, k * C:(k + 1) * C], T.x[:, k * C:(k + 1) * C]).then_inc(T.sem["ld%d" % k], 16)
        g.scalar.dma_start(T.y[:], T.x[:, rank * B:(rank + 1) * B]).then_inc(T.sem.own, 16)
        left = 0
        for k in range(4):
            g.wait_ge(T.sem["ld%d" % k], 16)
            if mids[2 * k] is not None:
                trs = []
                for q in (2 * k, 2 * k + 1):
                    rid, pid, _se = topo.addr(mids[q])
                    off_chip = topo.chip(mids[q]) != topo.chip(core)
                    trs.append(RemoteDMATransfer(
                        dst_ids=[DstId(rid=rid, pnc=pid)], dma_engine_mask=0x00FF if off_chip else 0xFF00,
                        remote_sem=T.sem.chunk, src=T.xs[:, q * Q:(q + 1) * Q], dst=T.quad[:]))
                    left += 8
                g.remote_dma_fused(trs, local_sem=T.sem.read)
            else:
                for r in range(8 * k, 8 * k + 8):
                    if r != rank:
                        rid, pid, _se = topo.addr(T.cores[r])
                        g.remote_dma(T.land[:], T.xs[:, r * B:(r + 1) * B], T.sem.arrived, T.sem.read, pid, rid, 0xFFFF)
                        left += 16
        g.wait_ge(T.sem.read, left)
        g.scalar.wait_ge(T.sem.own, 16)
        return

    leader = False
    if core in mids:
        q = mids.index(core)
        owners = [T.cores[r] for r in range(4 * q, 4 * q + 4)]
        leader = core in owners
        g.wait_ge(T.sem.chunk, 8)
        if leader:
            for j, dst in enumerate(owners):
                if dst != core:
                    rid, pid, _se = topo.addr(dst)
                    g.remote_dma(T.land[:], T.quad[:, j * B:(j + 1) * B], T.sem.arrived, T.sem.read, pid, rid, 0xFFFF)
            g.wait_ge(T.sem.read, 48)
        else:
            trs = []
            for j, dst in enumerate(owners):
                rid, pid, _se = topo.addr(dst)
                trs.append(RemoteDMATransfer(
                    dst_ids=[DstId(rid=rid, pnc=pid)], dma_engine_mask=0x3 << (2 * j),
                    remote_sem=T.sem.arrived, src=T.quad[:, j * B:(j + 1) * B], dst=T.land[:]))
            g.remote_dma_fused(trs, local_sem=T.sem.read)
            g.wait_ge(T.sem.read, 8)

    if leader:
        j = rank % 4
        g.sync.wait_ge(T.sem.chunk, 8)
        g.sync.dma_start(T.y[:], T.quad[:, j * B:(j + 1) * B]).then_inc(T.sem.stored, 16)
    else:
        mid = mids[rank // 4]
        on_chip = mid is None or topo.chip(mid) == topo.chip(core)
        g.sync.wait_ge(T.sem.arrived, 16 if on_chip else 2)
        g.sync.dma_start(T.y[:], T.land[:]).then_inc(T.sem.stored, 16)
    g.sync.wait_ge(T.sem.stored, 16)
